import numpy as np
import ml_dtypes


def mxq(x, axis, fmt="e4m3"):
    dtype, down = {"e4m3": (ml_dtypes.float8_e4m3fn, 7), "e5m2": (ml_dtypes.float8_e5m2, 14)}[fmt]
    v = np.moveaxis(np.asarray(x, np.float32).astype(ml_dtypes.bfloat16).astype(np.float64), axis, -1)
    blocks = v.reshape(v.shape[:-1] + (-1, 32))
    amax = np.abs(blocks).max(-1, keepdims=True)
    byte = np.maximum(np.where(amax > 0, np.frexp(amax)[1] - 1 + 127, 0) - down, 1)
    scale = np.exp2(byte - 127.0)
    codes = (blocks / scale).astype(np.float32).astype(dtype).astype(np.float64)
    return np.moveaxis((codes * scale).reshape(v.shape), -1, axis)


WIDE = False


def mx_kscale(k):
    if not WIDE:
        return np.ones(k)
    levels = np.array([10, -10, 5, -5, 0])
    if k % 512:
        return np.exp2(np.random.permutation(np.resize(levels, k // 32))).repeat(32)
    a = np.empty((k // 512, 16))
    for p in range(k // 512):
        a[p, :8] = np.random.permutation(np.resize(levels, 8))
        for g in range(8):
            far = levels[np.abs(levels - a[p, g]) >= 10]
            a[p, g + 8] = far[np.random.randint(len(far))]
    return np.exp2(a.ravel()).repeat(32)


def f64(x):
    return np.asarray(x).astype(np.float64)


def striped(idx):
    return np.tile(np.asarray(idx).reshape(-1, 16).T, (8, 1)).astype(np.uint16)


def unstriped(offs):
    return offs[:16].T.reshape(-1).astype(np.int64)


def striped8(idx):
    return np.asarray(idx).reshape(8, -1, 16).transpose(0, 2, 1).reshape(128, -1).astype(np.uint16)


def unstriped8(offs):
    return offs.reshape(8, 16, -1).transpose(0, 2, 1).reshape(8, -1).astype(np.int64)


def pick8(x, idx, run):
    r = np.arange(len(x))
    return x[r[:, None], idx[r % (8 * run) // run]]


E2M1 = np.array([0.0, 0.5, 1.0, 1.5, 2.0, 3.0, 4.0, 6.0, -0.0, -0.5, -1.0, -1.5, -2.0, -3.0, -4.0, -6.0])


def pack_weight(w, fmt):
    k, n = w.shape
    w = f64(np.asarray(w, np.float32).astype(ml_dtypes.bfloat16)).reshape(k // 32, 32, n)
    amax = np.abs(w).max(1)
    if fmt == "e4m3":
        byte = np.frexp(amax)[1] - 1 + 127 - 7
    else:
        mant, ex = np.frexp(amax / 6.0)
        byte = np.where(mant > 0.5, ex, ex - 1) + 127
    byte = np.clip(np.where(amax > 0, byte, 1), 1, 254)
    scaled = (w * np.exp2(127.0 - byte)[:, None, :]).reshape(k, n).astype(np.float32)
    by_word = np.ascontiguousarray(scaled.reshape(k // 512, 128, 4, n).transpose(0, 1, 3, 2))
    if fmt == "e4m3":
        words = by_word.astype(ml_dtypes.float8_e4m3fn).view(np.uint8)
    else:
        c = by_word.astype(ml_dtypes.float4_e2m1fn).view(np.uint8) & 0xF
        words = (c[..., 0::2] | (c[..., 1::2] << 4)).reshape(k // 512, 128, 2 * n)
    return np.ascontiguousarray(words), np.ascontiguousarray(byte.astype(np.uint8).reshape(k // 512, 16, n))


def unpack_weight(words, scales, fmt):
    g, _, n = scales.shape
    words = np.ascontiguousarray(words).reshape(g, 128, n, -1)
    if fmt == "e4m3":
        vals = words.view(ml_dtypes.float8_e4m3fn).astype(np.float64)
    else:
        nib = np.empty((g, 128, n, 4), np.uint8)
        nib[..., 0::2] = words & 0xF
        nib[..., 1::2] = words >> 4
        vals = E2M1[nib]
    vals = vals * np.repeat(np.exp2(scales.astype(np.float64) - 127.0), 8, axis=1)[..., None]
    return vals.transpose(0, 1, 3, 2).reshape(g * 512, n)


def sigmoid(v):
    return 1.0 / (1.0 + np.exp(-v))


K, R, F, T, J, M = 512, 128, 512, 2048, 512, 256


def setup_inputs():
    n = np.random.standard_normal
    idx = np.random.permutation(T)[:J]
    idx2 = np.stack([np.random.permutation(J)[:M] for _ in range(8)])
    idx3 = np.stack([np.random.permutation(J)[:M] for _ in range(8)])
    fk = mx_kscale(K)
    dtabp = pack_weight(n((K, T)) / fk[:, None], "e2m1")
    tabp = pack_weight(n((K, T)) / fk[:, None], "e2m1")
    return {
        "dtab_words": dtabp[0],
        "dtab_scales": dtabp[1],
        "tab_words": tabp[0],
        "tab_scales": tabp[1],
        "w1": (n((K, R)) * 1 / np.sqrt(K) * fk[:, None]).astype(np.float32),
        "gain": (np.random.uniform(0.5, 1.5, (R, 1))).astype(np.float32),
        "og": (np.random.uniform(0.5, 2.0, (R, 1))).astype(np.float32),
        "base": (0.3 * n((R, M))).astype(np.float32),
        "offs": striped(idx),
        "offs2": striped8(idx2),
        "offs3": striped8(idx3),
    }


def reference(dtab_words, dtab_scales, tab_words, tab_scales, w1, gain, og, base, offs, offs2, offs3):
    idx = unstriped(offs)
    idx2 = unstriped8(offs2)
    idx3 = unstriped8(offs3)
    dtabu = unpack_weight(dtab_words, dtab_scales, "e2m1")
    tabu = unpack_weight(tab_words, tab_scales, "e2m1")
    w1q = mxq(f64(w1), 0, "e4m3")
    tabidxg = tabu[:, idx]
    a = w1q.T @ tabidxg
    dtabidxg = dtabu[:, idx]
    ta = w1q.T @ dtabidxg
    h1 = a * f64(gain)
    th1 = ta * f64(gain)
    tu1 = pick8(th1, idx2, 16) * sigmoid(pick8(h1, idx3, 16)) + pick8(th1, idx3, 16) * sigmoid(pick8(h1, idx3, 16)) * (1.0 - sigmoid(pick8(h1, idx3, 16))) * pick8(h1, idx2, 16) - pick8(th1, idx3, 16) * sigmoid(pick8(h1, idx3, 16))
    y = tu1 * f64(og) + f64(base)
    return y

@@ -1,0 +1,120 @@
+from contextlib import ExitStack
+
+import concourse.mybir as mybir
+
+K, R, T, J, M = 512, 128, 2048, 512, 256
+FLOPS = 2 * 2 * K * R * J
+
+F32 = mybir.dt.float32
+BF16 = mybir.dt.bfloat16
+I32 = mybir.dt.int32
+U32 = mybir.dt.uint32
+U16 = mybir.dt.uint16
+U8 = mybir.dt.uint8
+FP8X4 = mybir.dt.float8_e4m3fn_x4
+FP4X4 = mybir.dt.float4_e2m1fn_x4
+ALU = mybir.AluOpType
+ACT = mybir.ActivationFunctionType
+
+P = 128
+PACK = 4
+
+
+def load_scales(nc, plane, scales):
+    for q in range(4):
+        nc.sync.dma_start(plane[32 * q : 32 * q + 4, :].bitcast(I32), scales[0, 4 * q : 4 * q + 4, :].bitcast(I32))
+
+
+def tile_attend_tpairgates_kernel(tc, dtab_words, dtab_scales, tab_words, tab_scales, w1, gain, og, base, offs, offs2, offs3, out):
+    nc = tc.nc
+    with ExitStack() as ctx:
+        sb = ctx.enter_context(tc.tile_pool(name="sb", bufs=1))
+        ps = ctx.enter_context(tc.psum_pool(name="ps", bufs=1))
+
+        idx = sb.tile([P, J // 16], U16, name="idx")
+        idx2 = sb.tile([P, M // 16], U16, name="idx2")
+        idx3 = sb.tile([P, M // 16], U16, name="idx3")
+        tab_w = sb.tile([P, T], U16, name="tab_w", align_bytes=64)
+        tab_s = sb.tile([P, T], U8, name="tab_s", align_bytes=64)
+        w_raw = sb.tile([P, PACK, R], F32, name="w_raw", tag="staged")
+        gain_c = sb.tile([P, 1], F32, name="gain_c")
+        og_c = sb.tile([P, 1], F32, name="og_c")
+        warm_in = sb.tile([P, 1], F32, name="warm_in", tag="later", align_bytes=64)
+        warm_out = sb.tile([P, 1], F32, name="warm_out", tag="late", align_bytes=64)
+        nc.gpsimd.memset(warm_in[:], 0.0)
+        nc.scalar.activation(warm_out[:], warm_in[:], ACT.Sigmoid)
+
+        nc.vector.memset(tab_s[:].bitcast(I32), 0)
+        dtab_s = sb.tile([P, T], U8, name="dtab_s", tag="later", align_bytes=64)
+        nc.vector.memset(dtab_s[:].bitcast(I32), 0)
+
+        dtab_w = sb.tile([P, T], U16, name="dtab_w", tag="late", align_bytes=64)
+        nc.sync.dma_start(idx[:], offs)
+        nc.sync.dma_start(idx3[:], offs3)
+        nc.sync.dma_start(tab_w[:].bitcast(I32), tab_words[0].bitcast(I32))
+        nc.sync.dma_start(idx2[:], offs2)
+        load_scales(nc, tab_s, tab_scales)
+        nc.sync.dma_start(w_raw[:], w1.rearrange("(p t) r -> p t r", t=PACK))
+        nc.sync.dma_start(dtab_w[:].bitcast(I32), dtab_words[0].bitcast(I32))
+        load_scales(nc, dtab_s, dtab_scales)
+        nc.gpsimd.dma_start(gain_c[:], gain)
+        nc.gpsimd.dma_start(og_c[:], og)
+
+        w_bf = sb.tile([P, R, PACK], BF16, name="w_bf", align_bytes=64)
+        nc.scalar.copy(w_bf[:], w_raw[:].rearrange("p t r -> p r t"))
+
+        base_t = sb.tile([P, M], F32, name="base_t", tag="staged")
+        nc.sync.dma_start(base_t[:], base)
+
+        g_tab_s = sb.tile([P, J], U8, name="g_tab_s", align_bytes=64)
+        g_tab_w = sb.tile([P, J], U16, name="g_tab_w", align_bytes=64)
+        g_dtab_s = sb.tile([P, J], U8, name="g_dtab_s", align_bytes=64)
+        g_dtab_w = sb.tile([P, J], U16, name="g_dtab_w", align_bytes=64)
+        w_codes = sb.tile([P, R], U32, name="w_codes", align_bytes=64)
+        w_scales = sb.tile([P, R], U8, name="w_scales", align_bytes=64)
+
+        nc.vector.tensor_copy(g_tab_w[:], tab_w[:].indirect(idx[:]))
+        nc.vector.tensor_copy(g_tab_s[:], tab_s[:].indirect(idx[:]))
+        nc.vector.quantize_mx(out=w_codes[:].bitcast(FP8X4), scales=w_scales[:], in_=w_bf[:].rearrange("p r t -> p (r t)"))
+
+        a_ps = ps.tile([P, J], F32, name="a_ps")
+        ta_ps = [ps.tile([P, J // 2], F32, name="ta_ps%d" % i) for i in range(2)]
+        nc.tensor.matmul_mx(out=a_ps[:], lhsT=w_codes[:].bitcast(FP8X4), lhsT_scale=w_scales[:],
+                            rhs=g_tab_w[:].bitcast(FP4X4), rhs_scale=g_tab_s[:], start=True, stop=True)
+        h1 = sb.tile([P, J], F32, name="h1")
+        nc.scalar.activation(h1[:], a_ps[:], ACT.Copy, scale=gain_c[:])
+        sig = sb.tile([P, M], F32, name="sig")
+        nc.scalar.activation(sig[:], h1[:].indirect(idx3[:]), ACT.Sigmoid)
+        pw = sb.tile([P, M], F32, name="pw")
+        nc.scalar.activation(pw[:], sig[:], ACT.Copy, scale=og_c[:])
+
+        nc.vector.tensor_copy(g_dtab_w[:], dtab_w[:].indirect(idx[:]))
+        th1 = sb.tile([P, J], F32, name="th1")
+        h2 = sb.tile([P, M], F32, name="h2", tag="late", align_bytes=64)
+        JH = J // 2
+        for i in range(2):
+            cols = slice(i * JH, (i + 1) * JH)
+            nc.vector.tensor_copy(g_dtab_s[:, cols], dtab_s[:].indirect(idx[:, i * JH // 16 : (i + 1) * JH // 16]))
+            nc.tensor.matmul_mx(out=ta_ps[i][:], lhsT=w_codes[:].bitcast(FP8X4), lhsT_scale=w_scales[:],
+                                rhs=g_dtab_w[:, cols].bitcast(FP4X4), rhs_scale=g_dtab_s[:, cols], start=True, stop=True)
+            nc.scalar.activation(th1[:, cols], ta_ps[i][:], ACT.Copy, scale=gain_c[:])
+            if i == 0:
+                nc.vector.tensor_copy(h2[:], h1[:].indirect(idx2[:]))
+
+        aa = sb.tile([P, M], F32, name="aa", tag="later", align_bytes=64)
+        qq = sb.tile([P, M], F32, name="qq")
+        nc.vector.scalar_tensor_tensor(aa[:], sig[:], 1.0, h2[:], ALU.subtract, ALU.mult)
+        nc.vector.scalar_tensor_tensor(qq[:], aa[:], 1.0, pw[:], ALU.add, ALU.mult)
+
+        xx = sb.tile([P, M], F32, name="xx")
+        yy = sb.tile([P, M], F32, name="yy")
+        nc.vector.tensor_tensor(yy[:], th1[:].indirect(idx2[:]), pw[:], ALU.mult)
+        nc.vector.tensor_tensor(xx[:], th1[:].indirect(idx3[:]), qq[:], ALU.mult)
+        H = M // 2
+        ww = [sb.tile([P, H], F32, name="ww%d" % i) for i in range(2)]
+        res = [sb.tile([P, H], F32, name="res%d" % i) for i in range(2)]
+        for i in range(2):
+            nc.vector.tensor_tensor(ww[i][:], base_t[:, i * H : (i + 1) * H], yy[:, i * H : (i + 1) * H], ALU.add)
+        for i, queue in enumerate((nc.scalar, nc.sync)):
+            nc.vector.tensor_tensor(res[i][:], ww[i][:], xx[:, i * H : (i + 1) * H], ALU.subtract)
+            queue.dma_start(out[:, i * H : (i + 1) * H], res[i][:])

@@ -36,34 +36,34 @@ def tile_attend_tpairgates_kernel(tc, dtab_words, dtab_scales, tab_words, tab_sc
         idx3 = sb.tile([P, M // 16], U16, name="idx3")
         tab_w = sb.tile([P, T], U16, name="tab_w", align_bytes=64)
         tab_s = sb.tile([P, T], U8, name="tab_s", align_bytes=64)
-        w_raw = sb.tile([P, PACK, R], F32, name="w_raw", tag="staged")
+        dtab_s = sb.tile([P, T], U8, name="dtab_s", align_bytes=64)
+        w_raw = sb.tile([P, PACK, R], F32, name="w_raw")
         gain_c = sb.tile([P, 1], F32, name="gain_c")
         og_c = sb.tile([P, 1], F32, name="og_c")
-        warm_in = sb.tile([P, 1], F32, name="warm_in", tag="later", align_bytes=64)
-        warm_out = sb.tile([P, 1], F32, name="warm_out", tag="late", align_bytes=64)
+        warm_in = sb.tile([P, 1], F32, name="warm_in")
+        warm_out = sb.tile([P, 1], F32, name="warm_out", align_bytes=64)
         nc.gpsimd.memset(warm_in[:], 0.0)
         nc.scalar.activation(warm_out[:], warm_in[:], ACT.Sigmoid)
 
         nc.vector.memset(tab_s[:].bitcast(I32), 0)
-        dtab_s = sb.tile([P, T], U8, name="dtab_s", tag="later", align_bytes=64)
         nc.vector.memset(dtab_s[:].bitcast(I32), 0)
 
-        dtab_w = sb.tile([P, T], U16, name="dtab_w", tag="late", align_bytes=64)
+        dtab_w = sb.tile([P, T], U16, name="dtab_w", align_bytes=64)
         nc.sync.dma_start(idx[:], offs)
-        nc.sync.dma_start(idx3[:], offs3)
         nc.sync.dma_start(tab_w[:].bitcast(I32), tab_words[0].bitcast(I32))
-        nc.sync.dma_start(idx2[:], offs2)
         load_scales(nc, tab_s, tab_scales)
         nc.sync.dma_start(w_raw[:], w1.rearrange("(p t) r -> p t r", t=PACK))
         nc.sync.dma_start(dtab_w[:].bitcast(I32), dtab_words[0].bitcast(I32))
         load_scales(nc, dtab_s, dtab_scales)
+        nc.sync.dma_start(idx3[:], offs3)
+        nc.sync.dma_start(idx2[:], offs2)
         nc.gpsimd.dma_start(gain_c[:], gain)
         nc.gpsimd.dma_start(og_c[:], og)
 
         w_bf = sb.tile([P, R, PACK], BF16, name="w_bf", align_bytes=64)
         nc.scalar.copy(w_bf[:], w_raw[:].rearrange("p t r -> p r t"))
 
-        base_t = sb.tile([P, M], F32, name="base_t", tag="staged")
+        base_t = sb.tile([P, M], F32, name="base_t")
         nc.sync.dma_start(base_t[:], base)
 
         g_tab_s = sb.tile([P, J], U8, name="g_tab_s", align_bytes=64)
@@ -90,7 +90,7 @@ def tile_attend_tpairgates_kernel(tc, dtab_words, dtab_scales, tab_words, tab_sc
 
         nc.vector.tensor_copy(g_dtab_w[:], dtab_w[:].indirect(idx[:]))
         th1 = sb.tile([P, J], F32, name="th1")
-        h2 = sb.tile([P, M], F32, name="h2", tag="late", align_bytes=64)
+        h2 = sb.tile([P, M], F32, name="h2")
         JH = J // 2
         for i in range(2):
             cols = slice(i * JH, (i + 1) * JH)
@@ -101,7 +101,7 @@ def tile_attend_tpairgates_kernel(tc, dtab_words, dtab_scales, tab_words, tab_sc
             if i == 0:
                 nc.vector.tensor_copy(h2[:], h1[:].indirect(idx2[:]))
 
-        aa = sb.tile([P, M], F32, name="aa", tag="later", align_bytes=64)
+        aa = sb.tile([P, M], F32, name="aa")
         qq = sb.tile([P, M], F32, name="qq")
         nc.vector.scalar_tensor_tensor(aa[:], sig[:], 1.0, h2[:], ALU.subtract, ALU.mult)
         nc.vector.scalar_tensor_tensor(qq[:], aa[:], 1.0, pw[:], ALU.add, ALU.mult)

@@ -18,11 +18,20 @@ ACT = mybir.ActivationFunctionType
 
 P = 128
 PACK = 4
+QUADRANT = 32
+SCALE_ROWS = QUADRANT * PACK // 32
+PER_COLUMN = 16
+MX_ALIGN = 64
+J_HALF = J // 2
+M_HALF = M // 2
 
 
-def load_scales(nc, plane, scales):
-    for q in range(4):
-        nc.sync.dma_start(plane[32 * q : 32 * q + 4, :].bitcast(I32), scales[0, 4 * q : 4 * q + 4, :].bitcast(I32))
+def load_scales(nc, scale_tile, scales):
+    for q in range(P // QUADRANT):
+        nc.sync.dma_start(
+            scale_tile[QUADRANT * q : QUADRANT * q + SCALE_ROWS, :].bitcast(I32),
+            scales[0, SCALE_ROWS * q : SCALE_ROWS * (q + 1), :].bitcast(I32),
+        )
 
 
 def tile_attend_tpairgates_kernel(tc, dtab_words, dtab_scales, tab_words, tab_scales, w1, gain, og, base, offs, offs2, offs3, out):
@@ -31,90 +40,92 @@ def tile_attend_tpairgates_kernel(tc, dtab_words, dtab_scales, tab_words, tab_sc
         sb = ctx.enter_context(tc.tile_pool(name="sb", bufs=1))
         ps = ctx.enter_context(tc.psum_pool(name="ps", bufs=1))
 
-        idx = sb.tile([P, J // 16], U16, name="idx")
-        idx2 = sb.tile([P, M // 16], U16, name="idx2")
-        idx3 = sb.tile([P, M // 16], U16, name="idx3")
-        tab_w = sb.tile([P, T], U16, name="tab_w", align_bytes=64)
-        tab_s = sb.tile([P, T], U8, name="tab_s", align_bytes=64)
-        dtab_s = sb.tile([P, T], U8, name="dtab_s", align_bytes=64)
+        idx = sb.tile([P, J // PER_COLUMN], U16, name="idx")
+        idx2 = sb.tile([P, M // PER_COLUMN], U16, name="idx2")
+        idx3 = sb.tile([P, M // PER_COLUMN], U16, name="idx3")
+        tab_w = sb.tile([P, T], U16, name="tab_w", align_bytes=MX_ALIGN)
+        tab_s = sb.tile([P, T], U8, name="tab_s", align_bytes=MX_ALIGN)
+        dtab_s = sb.tile([P, T], U8, name="dtab_s", align_bytes=MX_ALIGN)
         w_raw = sb.tile([P, PACK, R], F32, name="w_raw")
         gain_c = sb.tile([P, 1], F32, name="gain_c")
         og_c = sb.tile([P, 1], F32, name="og_c")
+
         warm_in = sb.tile([P, 1], F32, name="warm_in")
-        warm_out = sb.tile([P, 1], F32, name="warm_out", align_bytes=64)
+        warm_out = sb.tile([P, 1], F32, name="warm_out", align_bytes=MX_ALIGN)
         nc.gpsimd.memset(warm_in[:], 0.0)
         nc.scalar.activation(warm_out[:], warm_in[:], ACT.Sigmoid)
 
         nc.vector.memset(tab_s[:].bitcast(I32), 0)
         nc.vector.memset(dtab_s[:].bitcast(I32), 0)
 
-        dtab_w = sb.tile([P, T], U16, name="dtab_w", align_bytes=64)
+        dtab_w = sb.tile([P, T], U16, name="dtab_w", align_bytes=MX_ALIGN)
         nc.sync.dma_start(idx[:], offs)
         nc.sync.dma_start(tab_w[:].bitcast(I32), tab_words[0].bitcast(I32))
         load_scales(nc, tab_s, tab_scales)
         nc.sync.dma_start(w_raw[:], w1.rearrange("(p t) r -> p t r", t=PACK))
         nc.sync.dma_start(dtab_w[:].bitcast(I32), dtab_words[0].bitcast(I32))
+        nc.sync.dma_start(gain_c[:], gain)
         load_scales(nc, dtab_s, dtab_scales)
         nc.sync.dma_start(idx3[:], offs3)
         nc.sync.dma_start(idx2[:], offs2)
-        nc.gpsimd.dma_start(gain_c[:], gain)
-        nc.gpsimd.dma_start(og_c[:], og)
+        nc.sync.dma_start(og_c[:], og)
 
-        w_bf = sb.tile([P, R, PACK], BF16, name="w_bf", align_bytes=64)
+        w_bf = sb.tile([P, R, PACK], BF16, name="w_bf", align_bytes=MX_ALIGN)
         nc.scalar.copy(w_bf[:], w_raw[:].rearrange("p t r -> p r t"))
 
         base_t = sb.tile([P, M], F32, name="base_t")
         nc.sync.dma_start(base_t[:], base)
 
-        g_tab_s = sb.tile([P, J], U8, name="g_tab_s", align_bytes=64)
-        g_tab_w = sb.tile([P, J], U16, name="g_tab_w", align_bytes=64)
-        g_dtab_s = sb.tile([P, J], U8, name="g_dtab_s", align_bytes=64)
-        g_dtab_w = sb.tile([P, J], U16, name="g_dtab_w", align_bytes=64)
-        w_codes = sb.tile([P, R], U32, name="w_codes", align_bytes=64)
-        w_scales = sb.tile([P, R], U8, name="w_scales", align_bytes=64)
+        g_tab_s = sb.tile([P, J], U8, name="g_tab_s", align_bytes=MX_ALIGN)
+        g_tab_w = sb.tile([P, J], U16, name="g_tab_w", align_bytes=MX_ALIGN)
+        g_dtab_s = sb.tile([P, J], U8, name="g_dtab_s", align_bytes=MX_ALIGN)
+        g_dtab_w = sb.tile([P, J], U16, name="g_dtab_w", align_bytes=MX_ALIGN)
+        w_codes = sb.tile([P, R], U32, name="w_codes", align_bytes=MX_ALIGN)
+        w_scales = sb.tile([P, R], U8, name="w_scales", align_bytes=MX_ALIGN)
 
         nc.vector.tensor_copy(g_tab_w[:], tab_w[:].indirect(idx[:]))
         nc.vector.tensor_copy(g_tab_s[:], tab_s[:].indirect(idx[:]))
         nc.vector.quantize_mx(out=w_codes[:].bitcast(FP8X4), scales=w_scales[:], in_=w_bf[:].rearrange("p r t -> p (r t)"))
 
         a_ps = ps.tile([P, J], F32, name="a_ps")
-        ta_ps = [ps.tile([P, J // 2], F32, name="ta_ps%d" % i) for i in range(2)]
+        ta_ps = [ps.tile([P, J_HALF], F32, name="ta_ps%d" % half) for half in range(2)]
         nc.tensor.matmul_mx(out=a_ps[:], lhsT=w_codes[:].bitcast(FP8X4), lhsT_scale=w_scales[:],
                             rhs=g_tab_w[:].bitcast(FP4X4), rhs_scale=g_tab_s[:], start=True, stop=True)
         h1 = sb.tile([P, J], F32, name="h1")
         nc.scalar.activation(h1[:], a_ps[:], ACT.Copy, scale=gain_c[:])
         sig = sb.tile([P, M], F32, name="sig")
         nc.scalar.activation(sig[:], h1[:].indirect(idx3[:]), ACT.Sigmoid)
-        pw = sb.tile([P, M], F32, name="pw")
-        nc.scalar.activation(pw[:], sig[:], ACT.Copy, scale=og_c[:])
+        coef2 = sb.tile([P, M], F32, name="coef2")
+        nc.scalar.activation(coef2[:], sig[:], ACT.Copy, scale=og_c[:])
 
         nc.vector.tensor_copy(g_dtab_w[:], dtab_w[:].indirect(idx[:]))
         th1 = sb.tile([P, J], F32, name="th1")
-        h2 = sb.tile([P, M], F32, name="h2")
-        JH = J // 2
-        for i in range(2):
-            cols = slice(i * JH, (i + 1) * JH)
-            nc.vector.tensor_copy(g_dtab_s[:, cols], dtab_s[:].indirect(idx[:, i * JH // 16 : (i + 1) * JH // 16]))
-            nc.tensor.matmul_mx(out=ta_ps[i][:], lhsT=w_codes[:].bitcast(FP8X4), lhsT_scale=w_scales[:],
-                                rhs=g_dtab_w[:, cols].bitcast(FP4X4), rhs_scale=g_dtab_s[:, cols], start=True, stop=True)
-            nc.scalar.activation(th1[:, cols], ta_ps[i][:], ACT.Copy, scale=gain_c[:])
-            if i == 0:
-                nc.vector.tensor_copy(h2[:], h1[:].indirect(idx2[:]))
+        h1_at2 = sb.tile([P, M], F32, name="h1_at2")
+        for half in range(2):
+            slots = slice(half * J_HALF, (half + 1) * J_HALF)
+            entries = slice(half * J_HALF // PER_COLUMN, (half + 1) * J_HALF // PER_COLUMN)
+            nc.vector.tensor_copy(g_dtab_s[:, slots], dtab_s[:].indirect(idx[:, entries]))
+            nc.tensor.matmul_mx(out=ta_ps[half][:], lhsT=w_codes[:].bitcast(FP8X4), lhsT_scale=w_scales[:],
+                                rhs=g_dtab_w[:, slots].bitcast(FP4X4), rhs_scale=g_dtab_s[:, slots], start=True, stop=True)
+            nc.scalar.activation(th1[:, slots], ta_ps[half][:], ACT.Copy, scale=gain_c[:])
+            if half == 0:
+                nc.vector.tensor_copy(h1_at2[:], h1[:].indirect(idx2[:]))
 
-        aa = sb.tile([P, M], F32, name="aa")
-        qq = sb.tile([P, M], F32, name="qq")
-        nc.vector.scalar_tensor_tensor(aa[:], sig[:], 1.0, h2[:], ALU.subtract, ALU.mult)
-        nc.vector.scalar_tensor_tensor(qq[:], aa[:], 1.0, pw[:], ALU.add, ALU.mult)
+        inner = sb.tile([P, M], F32, name="inner")
+        coef3 = sb.tile([P, M], F32, name="coef3")
+        nc.vector.scalar_tensor_tensor(inner[:], sig[:], 1.0, h1_at2[:], ALU.subtract, ALU.mult)
+        nc.vector.scalar_tensor_tensor(coef3[:], inner[:], 1.0, coef2[:], ALU.add, ALU.mult)
 
-        xx = sb.tile([P, M], F32, name="xx")
-        yy = sb.tile([P, M], F32, name="yy")
-        nc.vector.tensor_tensor(yy[:], th1[:].indirect(idx2[:]), pw[:], ALU.mult)
-        nc.vector.tensor_tensor(xx[:], th1[:].indirect(idx3[:]), qq[:], ALU.mult)
-        H = M // 2
-        ww = [sb.tile([P, H], F32, name="ww%d" % i) for i in range(2)]
-        res = [sb.tile([P, H], F32, name="res%d" % i) for i in range(2)]
-        for i in range(2):
-            nc.vector.tensor_tensor(ww[i][:], base_t[:, i * H : (i + 1) * H], yy[:, i * H : (i + 1) * H], ALU.add)
-        for i, queue in enumerate((nc.scalar, nc.sync)):
-            nc.vector.tensor_tensor(res[i][:], ww[i][:], xx[:, i * H : (i + 1) * H], ALU.subtract)
-            queue.dma_start(out[:, i * H : (i + 1) * H], res[i][:])
+        term3 = sb.tile([P, M], F32, name="term3")
+        term2 = sb.tile([P, M], F32, name="term2")
+        nc.vector.tensor_tensor(term2[:], th1[:].indirect(idx2[:]), coef2[:], ALU.mult)
+        nc.vector.tensor_tensor(term3[:], th1[:].indirect(idx3[:]), coef3[:], ALU.mult)
+
+        partial = [sb.tile([P, M_HALF], F32, name="partial%d" % half) for half in range(2)]
+        res = [sb.tile([P, M_HALF], F32, name="res%d" % half) for half in range(2)]
+        picks = [slice(half * M_HALF, (half + 1) * M_HALF) for half in range(2)]
+        for half in range(2):
+            nc.vector.tensor_tensor(partial[half][:], base_t[:, picks[half]], term2[:, picks[half]], ALU.add)
+        for half, queue in enumerate((nc.scalar, nc.sync)):
+            nc.vector.tensor_tensor(res[half][:], partial[half][:], term3[:, picks[half]], ALU.subtract)
+            queue.dma_start(out[:, picks[half]], res[half][:])

from contextlib import ExitStack

import concourse.mybir as mybir

K, R, T, J, M = 512, 128, 2048, 512, 256
FLOPS = 2 * 2 * K * R * J

F32 = mybir.dt.float32
BF16 = mybir.dt.bfloat16
I32 = mybir.dt.int32
U32 = mybir.dt.uint32
U16 = mybir.dt.uint16
U8 = mybir.dt.uint8
FP8X4 = mybir.dt.float8_e4m3fn_x4
FP4X4 = mybir.dt.float4_e2m1fn_x4
ALU = mybir.AluOpType
ACT = mybir.ActivationFunctionType

P = 128
PACK = 4
QUADRANT = 32
SCALE_ROWS = QUADRANT * PACK // 32
PER_COLUMN = 16
MX_ALIGN = 64
J_HALF = J // 2
M_HALF = M // 2


def load_scales(nc, scale_tile, scales):
    for q in range(P // QUADRANT):
        nc.sync.dma_start(
            scale_tile[QUADRANT * q : QUADRANT * q + SCALE_ROWS, :].bitcast(I32),
            scales[0, SCALE_ROWS * q : SCALE_ROWS * (q + 1), :].bitcast(I32),
        )


def tile_attend_tpairgates_kernel(tc, dtab_words, dtab_scales, tab_words, tab_scales, w1, gain, og, base, offs, offs2, offs3, out):
    nc = tc.nc
    with ExitStack() as ctx:
        sb = ctx.enter_context(tc.tile_pool(name="sb", bufs=1))
        ps = ctx.enter_context(tc.psum_pool(name="ps", bufs=1))

        idx = sb.tile([P, J // PER_COLUMN], U16, name="idx")
        idx2 = sb.tile([P, M // PER_COLUMN], U16, name="idx2")
        idx3 = sb.tile([P, M // PER_COLUMN], U16, name="idx3")
        tab_w = sb.tile([P, T], U16, name="tab_w", align_bytes=MX_ALIGN)
        tab_s = sb.tile([P, T], U8, name="tab_s", align_bytes=MX_ALIGN)
        dtab_s = sb.tile([P, T], U8, name="dtab_s", align_bytes=MX_ALIGN)
        w_raw = sb.tile([P, PACK, R], F32, name="w_raw")
        gain_c = sb.tile([P, 1], F32, name="gain_c")
        og_c = sb.tile([P, 1], F32, name="og_c")

        warm_in = sb.tile([P, 1], F32, name="warm_in")
        warm_out = sb.tile([P, 1], F32, name="warm_out", align_bytes=MX_ALIGN)
        nc.gpsimd.memset(warm_in[:], 0.0)
        nc.scalar.activation(warm_out[:], warm_in[:], ACT.Sigmoid)

        nc.vector.memset(tab_s[:].bitcast(I32), 0)
        nc.vector.memset(dtab_s[:].bitcast(I32), 0)

        dtab_w = sb.tile([P, T], U16, name="dtab_w", align_bytes=MX_ALIGN)
        nc.sync.dma_start(idx[:], offs)
        nc.sync.dma_start(tab_w[:].bitcast(I32), tab_words[0].bitcast(I32))
        load_scales(nc, tab_s, tab_scales)
        nc.sync.dma_start(w_raw[:], w1.rearrange("(p t) r -> p t r", t=PACK))
        nc.sync.dma_start(dtab_w[:].bitcast(I32), dtab_words[0].bitcast(I32))
        nc.sync.dma_start(gain_c[:], gain)
        load_scales(nc, dtab_s, dtab_scales)
        nc.sync.dma_start(idx3[:], offs3)
        nc.sync.dma_start(idx2[:], offs2)
        nc.sync.dma_start(og_c[:], og)

        w_bf = sb.tile([P, R, PACK], BF16, name="w_bf", align_bytes=MX_ALIGN)
        nc.scalar.copy(w_bf[:], w_raw[:].rearrange("p t r -> p r t"))

        base_t = sb.tile([P, M], F32, name="base_t")
        nc.sync.dma_start(base_t[:], base)

        g_tab_s = sb.tile([P, J], U8, name="g_tab_s", align_bytes=MX_ALIGN)
        g_tab_w = sb.tile([P, J], U16, name="g_tab_w", align_bytes=MX_ALIGN)
        g_dtab_s = sb.tile([P, J], U8, name="g_dtab_s", align_bytes=MX_ALIGN)
        g_dtab_w = sb.tile([P, J], U16, name="g_dtab_w", align_bytes=MX_ALIGN)
        w_codes = sb.tile([P, R], U32, name="w_codes", align_bytes=MX_ALIGN)
        w_scales = sb.tile([P, R], U8, name="w_scales", align_bytes=MX_ALIGN)

        nc.vector.tensor_copy(g_tab_w[:], tab_w[:].indirect(idx[:]))
        nc.vector.tensor_copy(g_tab_s[:], tab_s[:].indirect(idx[:]))
        nc.vector.quantize_mx(out=w_codes[:].bitcast(FP8X4), scales=w_scales[:], in_=w_bf[:].rearrange("p r t -> p (r t)"))

        a_ps = ps.tile([P, J], F32, name="a_ps")
        ta_ps = [ps.tile([P, J_HALF], F32, name="ta_ps%d" % half) for half in range(2)]
        nc.tensor.matmul_mx(out=a_ps[:], lhsT=w_codes[:].bitcast(FP8X4), lhsT_scale=w_scales[:],
                            rhs=g_tab_w[:].bitcast(FP4X4), rhs_scale=g_tab_s[:], start=True, stop=True)
        h1 = sb.tile([P, J], F32, name="h1")
        nc.scalar.activation(h1[:], a_ps[:], ACT.Copy, scale=gain_c[:])
        sig = sb.tile([P, M], F32, name="sig")
        nc.scalar.activation(sig[:], h1[:].indirect(idx3[:]), ACT.Sigmoid)
        coef2 = sb.tile([P, M], F32, name="coef2")
        nc.scalar.activation(coef2[:], sig[:], ACT.Copy, scale=og_c[:])

        nc.vector.tensor_copy(g_dtab_w[:], dtab_w[:].indirect(idx[:]))
        th1 = sb.tile([P, J], F32, name="th1")
        h1_at2 = sb.tile([P, M], F32, name="h1_at2")
        for half in range(2):
            slots = slice(half * J_HALF, (half + 1) * J_HALF)
            entries = slice(half * J_HALF // PER_COLUMN, (half + 1) * J_HALF // PER_COLUMN)
            nc.vector.tensor_copy(g_dtab_s[:, slots], dtab_s[:].indirect(idx[:, entries]))
            nc.tensor.matmul_mx(out=ta_ps[half][:], lhsT=w_codes[:].bitcast(FP8X4), lhsT_scale=w_scales[:],
                                rhs=g_dtab_w[:, slots].bitcast(FP4X4), rhs_scale=g_dtab_s[:, slots], start=True, stop=True)
            nc.scalar.activation(th1[:, slots], ta_ps[half][:], ACT.Copy, scale=gain_c[:])
            if half == 0:
                nc.vector.tensor_copy(h1_at2[:], h1[:].indirect(idx2[:]))

        inner = sb.tile([P, M], F32, name="inner")
        coef3 = sb.tile([P, M], F32, name="coef3")
        nc.vector.scalar_tensor_tensor(inner[:], sig[:], 1.0, h1_at2[:], ALU.subtract, ALU.mult)
        nc.vector.scalar_tensor_tensor(coef3[:], inner[:], 1.0, coef2[:], ALU.add, ALU.mult)

        term3 = sb.tile([P, M], F32, name="term3")
        term2 = sb.tile([P, M], F32, name="term2")
        nc.vector.tensor_tensor(term2[:], th1[:].indirect(idx2[:]), coef2[:], ALU.mult)
        nc.vector.tensor_tensor(term3[:], th1[:].indirect(idx3[:]), coef3[:], ALU.mult)

        partial = [sb.tile([P, M_HALF], F32, name="partial%d" % half) for half in range(2)]
        res = [sb.tile([P, M_HALF], F32, name="res%d" % half) for half in range(2)]
        picks = [slice(half * M_HALF, (half + 1) * M_HALF) for half in range(2)]
        for half in range(2):
            nc.vector.tensor_tensor(partial[half][:], base_t[:, picks[half]], term2[:, picks[half]], ALU.add)
        for half, queue in enumerate((nc.scalar, nc.sync)):
            nc.vector.tensor_tensor(res[half][:], partial[half][:], term3[:, picks[half]], ALU.subtract)
            queue.dma_start(out[:, picks[half]], res[half][:])
